import numpy as np
import ml_dtypes


def mxq(x, axis, fmt="e4m3"):
    dtype, down = {"e4m3": (ml_dtypes.float8_e4m3fn, 7), "e5m2": (ml_dtypes.float8_e5m2, 14)}[fmt]
    v = np.moveaxis(np.asarray(x, np.float32).astype(ml_dtypes.bfloat16).astype(np.float64), axis, -1)
    blocks = v.reshape(v.shape[:-1] + (-1, 32))
    amax = np.abs(blocks).max(-1, keepdims=True)
    byte = np.maximum(np.where(amax > 0, np.frexp(amax)[1] - 1 + 127, 0) - down, 1)
    scale = np.exp2(byte - 127.0)
    codes = (blocks / scale).astype(np.float32).astype(dtype).astype(np.float64)
    return np.moveaxis((codes * scale).reshape(v.shape), -1, axis)


WIDE = False


def mx_kscale(k):
    if not WIDE:
        return np.ones(k)
    levels = np.array([10, -10, 5, -5, 0])
    if k % 512:
        return np.exp2(np.random.permutation(np.resize(levels, k // 32))).repeat(32)
    a = np.empty((k // 512, 16))
    for p in range(k // 512):
        a[p, :8] = np.random.permutation(np.resize(levels, 8))
        for g in range(8):
            far = levels[np.abs(levels - a[p, g]) >= 10]
            a[p, g + 8] = far[np.random.randint(len(far))]
    return np.exp2(a.ravel()).repeat(32)


def f64(x):
    return np.asarray(x).astype(np.float64)


def striped(idx):
    return np.tile(idx.reshape(-1, 16).T, (8, 1)).astype(np.uint16)


def unstriped(offs):
    return offs[:16].T.reshape(-1).astype(np.int64)


E2M1 = np.array([0.0, 0.5, 1.0, 1.5, 2.0, 3.0, 4.0, 6.0, -0.0, -0.5, -1.0, -1.5, -2.0, -3.0, -4.0, -6.0])


def pack_weight(w, fmt):
    k, n = w.shape
    w = f64(np.asarray(w, np.float32).astype(ml_dtypes.bfloat16)).reshape(k // 32, 32, n)
    amax = np.abs(w).max(1)
    if fmt == "e4m3":
        byte = np.frexp(amax)[1] - 1 + 127 - 7
    else:
        mant, ex = np.frexp(amax / 6.0)
        byte = np.where(mant > 0.5, ex, ex - 1) + 127
    byte = np.clip(np.where(amax > 0, byte, 1), 1, 254)
    scaled = (w * np.exp2(127.0 - byte)[:, None, :]).reshape(k, n).astype(np.float32)
    by_word = np.ascontiguousarray(scaled.reshape(k // 512, 128, 4, n).transpose(0, 1, 3, 2))
    if fmt == "e4m3":
        words = by_word.astype(ml_dtypes.float8_e4m3fn).view(np.uint8)
    else:
        c = by_word.astype(ml_dtypes.float4_e2m1fn).view(np.uint8) & 0xF
        words = (c[..., 0::2] | (c[..., 1::2] << 4)).reshape(k // 512, 128, 2 * n)
    return np.ascontiguousarray(words), np.ascontiguousarray(byte.astype(np.uint8).reshape(k // 512, 16, n))


def unpack_weight(words, scales, fmt):
    g, _, n = scales.shape
    words = np.ascontiguousarray(words).reshape(g, 128, n, -1)
    if fmt == "e4m3":
        vals = words.view(ml_dtypes.float8_e4m3fn).astype(np.float64)
    else:
        nib = np.empty((g, 128, n, 4), np.uint8)
        nib[..., 0::2] = words & 0xF
        nib[..., 1::2] = words >> 4
        vals = E2M1[nib]
    vals = vals * np.repeat(np.exp2(scales.astype(np.float64) - 127.0), 8, axis=1)[..., None]
    return vals.transpose(0, 1, 3, 2).reshape(g * 512, n)


def gelu(v):
    return 0.5 * v * (1.0 + np.tanh(np.sqrt(2.0 / np.pi) * (v + 0.044715 * v**3)))


def bf(x):
    return np.asarray(x, np.float32).astype(ml_dtypes.bfloat16)


def planes(Y):
    n, m = Y.shape
    b = f64(bf(Y)).reshape(n // 32, 32, m)
    amax = np.abs(b).max(1)
    byte = np.clip(np.where(amax > 0, np.frexp(amax)[1] - 1 + 127 - 7, 1), 1, 254)
    codes = (b * np.exp2(127.0 - byte)[:, None, :]).reshape(n, m).astype(np.float32).astype(ml_dtypes.float8_e4m3fn).view(np.uint8)
    words = codes.reshape(n // 512, 128, 4, m).transpose(0, 1, 3, 2)
    return np.ascontiguousarray(words), np.ascontiguousarray(byte.astype(np.uint8).reshape(n // 512, 16, m))


K, H, N, T, S, T2, P = 1024, 1024, 512, 4096, 1024, 2048, 1024

def setup_inputs():
    n = np.random.standard_normal
    s = mx_kscale(K)[:, None]
    u = mx_kscale(H)[:, None]
    size = np.exp(0.8 * n(N))
    tab_words, tab_scales = pack_weight(n((K, T)) * s, "e4m3")
    wa_words, wa_scales = pack_weight(n((H, N)) / u * size / np.sqrt(H), "e2m1")
    return {
        "tab_words": tab_words, "tab_scales": tab_scales,
        "offs": striped(np.random.permutation(T)[:S]),
        "offs2": striped(np.random.permutation(T2)[:S]),
        "offs3": striped(np.random.permutation(T2)[:P]),
        "w1": (n((K, H)) / s * u.T / np.sqrt(K)).astype(np.float32),
        "b1": (0.5 * n(H) * u[:, 0]).astype(np.float32),
        "crowd": np.exp(0.4 * n((H, S))).astype(np.float32),
        "page0": (n((H, T2)) * u).astype(np.float32),
        "wa_words": wa_words, "wa_scales": wa_scales,
        "ba": (0.5 * n(N) * size).astype(np.float32),
        "wb": (n((H, N)) / u / np.sqrt(H)).astype(np.float32),
        "cap": (np.random.uniform(1.2, 2.2, N) * size).astype(np.float32),
    }

def reference(tab_words, tab_scales, offs, offs2, offs3, w1, b1, crowd, page0, wa_words, wa_scales, ba, wb, cap):
    v = unpack_weight(tab_words, tab_scales, "e4m3")[:, unstriped(offs)]
    h = (mxq(f64(w1), 0, "e4m3").T @ v) + f64(b1)[:, None]
    page = f64(page0).copy()
    l2 = unstriped(offs2)
    page[:, l2] = page[:, l2] + f64(crowd) * h
    x = mxq(page[:, unstriped(offs3)], 0, "e4m3")
    ya = (unpack_weight(wa_words, wa_scales, "e2m1").T @ x) + f64(ba)[:, None]
    yb = f64(cap)[:, None] * np.tanh(mxq(f64(wb), 0, "e4m3").T @ x)
    y = np.maximum(ya, yb)
    words, scales = planes(y)
    return y, words, scales

@@ -1,0 +1,214 @@
+from contextlib import ExitStack
+
+import concourse.mybir as mybir
+
+K, H, N, T, S, T2, M = 1024, 1024, 512, 4096, 1024, 2048, 1024
+FLOPS = 2 * K * H * S + 2 * 2 * H * N * M
+
+F32 = mybir.dt.float32
+BF16 = mybir.dt.bfloat16
+I32 = mybir.dt.int32
+U32 = mybir.dt.uint32
+U16 = mybir.dt.uint16
+U8 = mybir.dt.uint8
+FP8X4 = mybir.dt.float8_e4m3fn_x4
+FP4X4 = mybir.dt.float4_e2m1fn_x4
+ALU = mybir.AluOpType
+ACT = mybir.ActivationFunctionType
+
+P = 128
+PACK = 4
+K_PASS = P * PACK
+BANK = 512
+PER_COL = 16
+CHUNKS = (256, 256, 256, 128, 128)
+SLICE_GROUPS = ((0,), (1,), (2, 3), (4, 5), (6, 7))
+
+
+def tile_list_door_force_record_kernel(
+    tc, tab_words, tab_scales, offs, offs2, offs3, w1, b1, crowd, page0, wa_words, wa_scales, ba, wb, cap,
+    out_0, out_1, out_2,
+):
+    nc = tc.nc
+    with ExitStack() as ctx:
+        keep = ctx.enter_context(tc.tile_pool(name="keep", bufs=1))
+        ring = ctx.enter_context(tc.tile_pool(name="ring", bufs=2))
+        psum = ctx.enter_context(tc.psum_pool(name="psum", bufs=8))
+
+        idx1 = keep.tile([P, S // PER_COL], U16, name="idx1")
+        idx2 = keep.tile([P, S // PER_COL], U16, name="idx2")
+        idx3 = keep.tile([P, M // PER_COL], U16, name="idx3")
+        b1_sb = keep.tile([P, 2, PACK], F32, name="b1_sb")
+        ba_sb = keep.tile([P, PACK], F32, name="ba_sb")
+        cap_sb = keep.tile([P, PACK], F32, name="cap_sb")
+
+        tab_w = [keep.tile([P, T], U32, name="tab_w%d" % a, align_bytes=64) for a in range(2)]
+        tab_s = keep.tile([P, T], U8, name="tab_s", align_bytes=64)
+        v_w = [keep.tile([P, S], U32, name="v_w%d" % a, align_bytes=64) for a in range(2)]
+        v_s = keep.tile([P, S], U8, name="v_s", align_bytes=64)
+        pages = [keep.tile([P, T2], F32, name="page%d" % s, align_bytes=64) for s in range(8)]
+        wa_raw = keep.tile([P, 2, 2 * N], U8, name="wa_raw", align_bytes=64)
+        wa_sraw = keep.tile([P, 2, N], U8, name="wa_sraw", align_bytes=64)
+        wa_w = keep.tile([P, 2, PACK, 2 * P], U8, name="wa_w", align_bytes=64)
+        wa_s = keep.tile([P, 2, PACK, P], U8, name="wa_s", align_bytes=64)
+        y_w = keep.tile([P, M], U32, name="y_w", align_bytes=64)
+        y_s = keep.tile([P, M], U8, name="y_s", align_bytes=64)
+
+        def quantised_weight(name, block):
+            raw = ring.tile([P, PACK, K_PASS], F32, name="w_raw", tag="w_raw", bufs=2)
+            nc.sync.dma_start(out=raw[:], in_=block.rearrange("(p j) c -> p j c", j=PACK))
+            grouped = ring.tile([P, K_PASS * PACK], BF16, name="w_grouped", tag="w_grouped", bufs=2, align_bytes=64)
+            nc.scalar.copy(
+                out=grouped[:].rearrange("p (t m j) -> p m t j", t=PACK, j=PACK),
+                in_=raw[:].rearrange("p j (m t) -> p m t j", t=PACK),
+            )
+            codes = keep.tile([P, K_PASS], U32, name=name + "_w", align_bytes=64)
+            scales = keep.tile([P, K_PASS], U8, name=name + "_s", align_bytes=64)
+            nc.vector.quantize_mx(out=codes[:].bitcast(FP8X4), scales=scales[:], in_=grouped[:])
+            return codes, scales
+
+        def load_table(a):
+            nc.sync.dma_start(
+                out=tab_w[a][:].bitcast(I32), in_=tab_words[a].rearrange("p n i -> p (n i)").bitcast(I32)
+            )
+
+        def load_page(s):
+            b, t = divmod(s, PACK)
+            rows = page0[b * K_PASS : (b + 1) * K_PASS, :].rearrange("(p t) c -> p t c", t=PACK)
+            nc.sync.dma_start(out=pages[s][:], in_=rows[:, t, :])
+
+        nc.vector.memset(tab_s[:].bitcast(I32), 0)
+        nc.vector.memset(wa_sraw[:].rearrange("p a n -> p (a n)").bitcast(I32), 0)
+        nc.sync.dma_start(out=wa_raw[:].bitcast(I32), in_=wa_words.rearrange("a p c -> p a c").bitcast(I32))
+        load_table(0)
+        nc.sync.dma_start(idx1[:], offs)
+        for q in range(4):
+            nc.scalar.dma_start(
+                out=tab_s[32 * q : 32 * q + 8, :].bitcast(I32), in_=tab_scales[:, 4 * q : 4 * q + 4, :].bitcast(I32)
+            )
+        for q in range(4):
+            nc.scalar.dma_start(
+                out=wa_sraw[32 * q : 32 * q + 4].bitcast(I32),
+                in_=wa_scales[:, 4 * q : 4 * q + 4, :].rearrange("a r n -> r a n").bitcast(I32),
+            )
+        for a in range(2):
+            nc.vector.tensor_copy(
+                out=wa_w[:, a].rearrange("p t (m e) -> p t m e", e=2),
+                in_=wa_raw[:, a].rearrange("p (m t e) -> p t m e", t=PACK, e=2),
+            )
+        nc.vector.tensor_copy(out=wa_s[:], in_=wa_sraw[:].rearrange("p a (m t) -> p a t m", t=PACK))
+        nc.vector.tensor_copy(v_s[:], tab_s[:].indirect(idx1[:]))
+        nc.vector.tensor_copy(v_w[0][:], tab_w[0][:].indirect(idx1[:]))
+        w1_q = {}
+        for a in range(2):
+            w1_q[a, 0] = quantised_weight("w1_%d0" % a, w1[a * K_PASS : (a + 1) * K_PASS, 0:K_PASS])
+        load_table(1)
+        nc.vector.tensor_copy(v_w[1][:], tab_w[1][:].indirect(idx1[:]))
+        nc.sync.dma_start(idx2[:], offs2)
+        nc.sync.dma_start(out=b1_sb[:], in_=b1.rearrange("(b p t) -> p b t", b=2, t=PACK))
+
+        wb_q = {}
+        for group in SLICE_GROUPS:
+            b, t0 = divmod(group[0], PACK)
+            old = {}
+            for s in group:
+                load_page(s)
+                old[s] = ring.tile([P, S], F32, name="old", tag="picked", bufs=3, align_bytes=64)
+                nc.vector.tensor_copy(old[s][:], pages[s][:].indirect(idx2[:]))
+            ch = ring.tile([P, len(group), S], F32, name="ch", tag="ch", bufs=3)
+            rows = crowd[b * K_PASS : (b + 1) * K_PASS, :].rearrange("(p t) c -> p t c", t=PACK)
+            nc.sync.dma_start(out=ch[:], in_=rows[:, t0 : t0 + len(group), :])
+            for i, s in enumerate(group):
+                t = s % PACK
+                for j0 in range(0, S, BANK):
+                    cols = slice(j0, j0 + BANK)
+                    acc = psum.tile([P, BANK], F32, name="acc", tag="acc")
+                    for a in range(2):
+                        codes, scales = w1_q[a, b]
+                        nc.tensor.matmul_mx(
+                            out=acc[:],
+                            lhsT=codes[:, t * P : (t + 1) * P].bitcast(FP8X4),
+                            lhsT_scale=scales[:, t * P : (t + 1) * P],
+                            rhs=v_w[a][:, cols].bitcast(FP8X4),
+                            rhs_scale=v_s[4 * a :, cols],
+                            start=(a == 0),
+                            stop=(a == 1),
+                        )
+                    nc.vector.scalar_tensor_tensor(
+                        out=ch[:, i, cols], in0=acc[:], scalar=b1_sb[:, b, t : t + 1], in1=ch[:, i, cols],
+                        op0=ALU.add, op1=ALU.mult,
+                    )
+            for i, s in enumerate(group):
+                nc.vector.tensor_tensor(pages[s][:].indirect(idx2[:]), old[s][:], ch[:, i, :], ALU.add)
+            if group[-1] == 3:
+                for a in range(2):
+                    w1_q[a, 1] = quantised_weight("w1_%d1" % a, w1[a * K_PASS : (a + 1) * K_PASS, K_PASS:])
+            if group[-1] == 5:
+                nc.sync.dma_start(idx3[:], offs3)
+                nc.sync.dma_start(out=ba_sb[:], in_=ba.rearrange("(p t) -> p t", t=PACK))
+                nc.sync.dma_start(out=cap_sb[:], in_=cap.rearrange("(p t) -> p t", t=PACK))
+                for a in range(2):
+                    wb_q[a] = quantised_weight("wb_%d" % a, wb[a * K_PASS : (a + 1) * K_PASS, :])
+
+        out_rows = out_0.rearrange("(p t) m -> p t m", t=PACK)
+        out_words = out_1[0].rearrange("p m t -> p (m t)").bitcast(I32)
+        out_scales = out_2[0].bitcast(I32)
+        m0 = 0
+        for w in CHUNKS:
+            cols = slice(m0, m0 + w)
+            banks = [psum.tile([P, 2, w], F32, name="acc", tag="acc") for t in range(PACK)]
+            for b in range(2):
+                x = ring.tile([P, PACK, w], BF16, name="x", tag="picked", bufs=3, align_bytes=64)
+                for t in range(PACK):
+                    nc.vector.tensor_copy(
+                        x[:, t, :], pages[PACK * b + t][:].indirect(idx3[:, m0 // PER_COL : (m0 + w) // PER_COL])
+                    )
+                x_grouped = ring.tile([P, w * PACK], BF16, name="x_grouped", tag="x_grouped", bufs=2, align_bytes=64)
+                nc.scalar.copy(
+                    out=x_grouped[:].rearrange("p (c i t) -> p c t i", i=4, t=PACK),
+                    in_=x[:].rearrange("p t (c i) -> p c t i", i=4),
+                )
+                x_w = ring.tile([P, w], U32, name="x_w", tag="x_w", bufs=3, align_bytes=64)
+                x_s = ring.tile([P, w], U8, name="x_s", tag="x_s", bufs=3, align_bytes=64)
+                nc.vector.quantize_mx(out=x_w[:].bitcast(FP8X4), scales=x_s[:], in_=x_grouped[:])
+                codes, scales = wb_q[b]
+                for t in range(PACK):
+                    nc.tensor.matmul_mx(
+                        out=banks[t][:, 0, :],
+                        lhsT=codes[:, t * P : (t + 1) * P].bitcast(FP8X4),
+                        lhsT_scale=scales[:, t * P : (t + 1) * P],
+                        rhs=x_w[:].bitcast(FP8X4),
+                        rhs_scale=x_s[:],
+                        start=(b == 0),
+                        stop=False,
+                    )
+                    nc.tensor.matmul_mx(
+                        out=banks[t][:, 1, :],
+                        lhsT=wa_w[:, b, t, :].bitcast(FP4X4),
+                        lhsT_scale=wa_s[:, b, t, :],
+                        rhs=x_w[:].bitcast(FP8X4),
+                        rhs_scale=x_s[:],
+                        start=False,
+                        stop=(b == 1),
+                    )
+            y = ring.tile([P, PACK, w], F32, name="y", tag="y", bufs=2, align_bytes=64)
+            for t in range(PACK):
+                yb = ring.tile([P, w], F32, name="yb", tag="yb", bufs=4)
+                nc.scalar.activation(out=yb[:], in_=banks[t][:, 0, :], func=ACT.Tanh)
+                nc.scalar.activation(out=yb[:], in_=yb[:], func=ACT.Copy, scale=cap_sb[:, t : t + 1])
+                nc.vector.scalar_tensor_tensor(
+                    out=y[:, t, :], in0=banks[t][:, 1, :], scalar=ba_sb[:, t : t + 1], in1=yb[:],
+                    op0=ALU.add, op1=ALU.max,
+                )
+            nc.sync.dma_start(out=out_rows[:, :, cols], in_=y[:])
+            y_grouped = ring.tile([P, w * PACK], BF16, name="y_grouped", tag="y_grouped", bufs=2, align_bytes=64)
+            nc.scalar.copy(
+                out=y_grouped[:].rearrange("p (c i t) -> p c t i", i=4, t=PACK),
+                in_=y[:].rearrange("p t (c i) -> p c t i", i=4),
+            )
+            nc.vector.quantize_mx(out=y_w[:, cols].bitcast(FP8X4), scales=y_s[:, cols], in_=y_grouped[:])
+            nc.sync.dma_start(out=out_words[:, cols], in_=y_w[:, cols].bitcast(I32))
+            m0 = m0 + w
+        for q in range(4):
+            queue = nc.scalar if q % 2 else nc.sync
+            queue.dma_start(out=out_scales[4 * q : 4 * q + 4, :], in_=y_s[32 * q : 32 * q + 4, :].bitcast(I32))

@@ -22,7 +22,6 @@ K_PASS = P * PACK
 BANK = 512
 PER_COL = 16
 CHUNKS = (256, 256, 256, 128, 128)
-SLICE_GROUPS = ((0,), (1,), (2, 3), (4, 5), (6, 7))
 
 
 def tile_list_door_force_record_kernel(
@@ -108,42 +107,50 @@ def tile_list_door_force_record_kernel(
         nc.sync.dma_start(out=b1_sb[:], in_=b1.rearrange("(b p t) -> p b t", b=2, t=PACK))
 
         wb_q = {}
-        for group in SLICE_GROUPS:
-            b, t0 = divmod(group[0], PACK)
-            old = {}
-            for s in group:
-                load_page(s)
-                old[s] = ring.tile([P, S], F32, name="old", tag="picked", bufs=3, align_bytes=64)
-                nc.vector.tensor_copy(old[s][:], pages[s][:].indirect(idx2[:]))
-            ch = ring.tile([P, len(group), S], F32, name="ch", tag="ch", bufs=3)
+        olds = {}
+        for s in range(8):
+            b, t = divmod(s, PACK)
+            for ahead in {0: (0,), 1: (1, 2), 7: ()}.get(s, (s + 1,)):
+                load_page(ahead)
+                olds[ahead] = ring.tile([P, S], F32, name="old", tag="picked", bufs=2, align_bytes=64)
+                nc.vector.tensor_copy(olds[ahead][:], pages[ahead][:].indirect(idx2[:]))
+            old = olds[s]
+            ch = ring.tile([P, S], F32, name="ch", tag="ch", bufs=4)
             rows = crowd[b * K_PASS : (b + 1) * K_PASS, :].rearrange("(p t) c -> p t c", t=PACK)
-            nc.sync.dma_start(out=ch[:], in_=rows[:, t0 : t0 + len(group), :])
-            for i, s in enumerate(group):
-                t = s % PACK
-                for j0 in range(0, S, BANK):
-                    cols = slice(j0, j0 + BANK)
-                    acc = psum.tile([P, BANK], F32, name="acc", tag="acc")
-                    for a in range(2):
-                        codes, scales = w1_q[a, b]
-                        nc.tensor.matmul_mx(
-                            out=acc[:],
-                            lhsT=codes[:, t * P : (t + 1) * P].bitcast(FP8X4),
-                            lhsT_scale=scales[:, t * P : (t + 1) * P],
-                            rhs=v_w[a][:, cols].bitcast(FP8X4),
-                            rhs_scale=v_s[4 * a :, cols],
-                            start=(a == 0),
-                            stop=(a == 1),
-                        )
+            nc.sync.dma_start(out=ch[:], in_=rows[:, t, :])
+            if s > 0:
+                h = ring.tile([P, S], F32, name="h", tag="h", bufs=2)
+            for j0 in range(0, S, BANK):
+                cols = slice(j0, j0 + BANK)
+                acc = psum.tile([P, BANK], F32, name="acc", tag="acc")
+                for a in range(2):
+                    codes, scales = w1_q[a, b]
+                    nc.tensor.matmul_mx(
+                        out=acc[:],
+                        lhsT=codes[:, t * P : (t + 1) * P].bitcast(FP8X4),
+                        lhsT_scale=scales[:, t * P : (t + 1) * P],
+                        rhs=v_w[a][:, cols].bitcast(FP8X4),
+                        rhs_scale=v_s[4 * a :, cols],
+                        start=(a == 0),
+                        stop=(a == 1),
+                    )
+                if s == 0:
                     nc.vector.scalar_tensor_tensor(
-                        out=ch[:, i, cols], in0=acc[:], scalar=b1_sb[:, b, t : t + 1], in1=ch[:, i, cols],
+                        out=ch[:, cols], in0=acc[:], scalar=b1_sb[:, b, t : t + 1], in1=ch[:, cols],
                         op0=ALU.add, op1=ALU.mult,
                     )
-            for i, s in enumerate(group):
-                nc.vector.tensor_tensor(pages[s][:].indirect(idx2[:]), old[s][:], ch[:, i, :], ALU.add)
-            if group[-1] == 3:
+                else:
+                    nc.scalar.activation(out=h[:, cols], in_=acc[:], func=ACT.Identity, bias=b1_sb[:, b, t : t + 1])
+            if s == 0:
+                nc.vector.tensor_tensor(pages[s][:].indirect(idx2[:]), old[:], ch[:], ALU.add)
+            else:
+                nc.gpsimd.tensor_tensor(ch[:], h[:], ch[:], ALU.mult)
+                nc.gpsimd.tensor_tensor(ch[:], old[:], ch[:], ALU.add)
+                nc.vector.tensor_copy(pages[s][:].indirect(idx2[:]), ch[:])
+            if s == 2:
                 for a in range(2):
                     w1_q[a, 1] = quantised_weight("w1_%d1" % a, w1[a * K_PASS : (a + 1) * K_PASS, K_PASS:])
-            if group[-1] == 5:
+            if s == 5:
                 nc.sync.dma_start(idx3[:], offs3)
                 nc.sync.dma_start(out=ba_sb[:], in_=ba.rearrange("(p t) -> p t", t=PACK))
                 nc.sync.dma_start(out=cap_sb[:], in_=cap.rearrange("(p t) -> p t", t=PACK))
@@ -158,7 +165,7 @@ def tile_list_door_force_record_kernel(
             cols = slice(m0, m0 + w)
             banks = [psum.tile([P, 2, w], F32, name="acc", tag="acc") for t in range(PACK)]
             for b in range(2):
-                x = ring.tile([P, PACK, w], BF16, name="x", tag="picked", bufs=3, align_bytes=64)
+                x = ring.tile([P, PACK, w], BF16, name="x", tag="picked", bufs=2, align_bytes=64)
                 for t in range(PACK):
                     nc.vector.tensor_copy(
                         x[:, t, :], pages[PACK * b + t][:].indirect(idx3[:, m0 // PER_COL : (m0 + w) // PER_COL])

from contextlib import ExitStack

import concourse.mybir as mybir

K, H, N, T, S, T2, M = 1024, 1024, 512, 4096, 1024, 2048, 1024
FLOPS = 2 * K * H * S + 2 * 2 * H * N * M

F32 = mybir.dt.float32
BF16 = mybir.dt.bfloat16
I32 = mybir.dt.int32
U32 = mybir.dt.uint32
U16 = mybir.dt.uint16
U8 = mybir.dt.uint8
FP8X4 = mybir.dt.float8_e4m3fn_x4
FP4X4 = mybir.dt.float4_e2m1fn_x4
ALU = mybir.AluOpType
ACT = mybir.ActivationFunctionType

P = 128
PACK = 4
K_PASS = P * PACK
BANK = 512
PER_COL = 16
CHUNKS = (256, 256, 256, 128, 128)


def tile_list_door_force_record_kernel(
    tc, tab_words, tab_scales, offs, offs2, offs3, w1, b1, crowd, page0, wa_words, wa_scales, ba, wb, cap,
    out_0, out_1, out_2,
):
    nc = tc.nc
    with ExitStack() as ctx:
        keep = ctx.enter_context(tc.tile_pool(name="keep", bufs=1))
        ring = ctx.enter_context(tc.tile_pool(name="ring", bufs=2))
        psum = ctx.enter_context(tc.psum_pool(name="psum", bufs=8))

        idx1 = keep.tile([P, S // PER_COL], U16, name="idx1")
        idx2 = keep.tile([P, S // PER_COL], U16, name="idx2")
        idx3 = keep.tile([P, M // PER_COL], U16, name="idx3")
        b1_sb = keep.tile([P, 2, PACK], F32, name="b1_sb")
        ba_sb = keep.tile([P, PACK], F32, name="ba_sb")
        cap_sb = keep.tile([P, PACK], F32, name="cap_sb")

        tab_w = [keep.tile([P, T], U32, name="tab_w%d" % a, align_bytes=64) for a in range(2)]
        tab_s = keep.tile([P, T], U8, name="tab_s", align_bytes=64)
        v_w = [keep.tile([P, S], U32, name="v_w%d" % a, align_bytes=64) for a in range(2)]
        v_s = keep.tile([P, S], U8, name="v_s", align_bytes=64)
        pages = [keep.tile([P, T2], F32, name="page%d" % s, align_bytes=64) for s in range(8)]
        wa_raw = keep.tile([P, 2, 2 * N], U8, name="wa_raw", align_bytes=64)
        wa_sraw = keep.tile([P, 2, N], U8, name="wa_sraw", align_bytes=64)
        wa_w = keep.tile([P, 2, PACK, 2 * P], U8, name="wa_w", align_bytes=64)
        wa_s = keep.tile([P, 2, PACK, P], U8, name="wa_s", align_bytes=64)
        y_w = keep.tile([P, M], U32, name="y_w", align_bytes=64)
        y_s = keep.tile([P, M], U8, name="y_s", align_bytes=64)

        def quantised_weight(name, block):
            raw = ring.tile([P, PACK, K_PASS], F32, name="w_raw", tag="w_raw", bufs=2)
            nc.sync.dma_start(out=raw[:], in_=block.rearrange("(p j) c -> p j c", j=PACK))
            grouped = ring.tile([P, K_PASS * PACK], BF16, name="w_grouped", tag="w_grouped", bufs=2, align_bytes=64)
            nc.scalar.copy(
                out=grouped[:].rearrange("p (t m j) -> p m t j", t=PACK, j=PACK),
                in_=raw[:].rearrange("p j (m t) -> p m t j", t=PACK),
            )
            codes = keep.tile([P, K_PASS], U32, name=name + "_w", align_bytes=64)
            scales = keep.tile([P, K_PASS], U8, name=name + "_s", align_bytes=64)
            nc.vector.quantize_mx(out=codes[:].bitcast(FP8X4), scales=scales[:], in_=grouped[:])
            return codes, scales

        def load_table(a):
            nc.sync.dma_start(
                out=tab_w[a][:].bitcast(I32), in_=tab_words[a].rearrange("p n i -> p (n i)").bitcast(I32)
            )

        def load_page(s):
            b, t = divmod(s, PACK)
            rows = page0[b * K_PASS : (b + 1) * K_PASS, :].rearrange("(p t) c -> p t c", t=PACK)
            nc.sync.dma_start(out=pages[s][:], in_=rows[:, t, :])

        nc.vector.memset(tab_s[:].bitcast(I32), 0)
        nc.vector.memset(wa_sraw[:].rearrange("p a n -> p (a n)").bitcast(I32), 0)
        nc.sync.dma_start(out=wa_raw[:].bitcast(I32), in_=wa_words.rearrange("a p c -> p a c").bitcast(I32))
        load_table(0)
        nc.sync.dma_start(idx1[:], offs)
        for q in range(4):
            nc.scalar.dma_start(
                out=tab_s[32 * q : 32 * q + 8, :].bitcast(I32), in_=tab_scales[:, 4 * q : 4 * q + 4, :].bitcast(I32)
            )
        for q in range(4):
            nc.scalar.dma_start(
                out=wa_sraw[32 * q : 32 * q + 4].bitcast(I32),
                in_=wa_scales[:, 4 * q : 4 * q + 4, :].rearrange("a r n -> r a n").bitcast(I32),
            )
        for a in range(2):
            nc.vector.tensor_copy(
                out=wa_w[:, a].rearrange("p t (m e) -> p t m e", e=2),
                in_=wa_raw[:, a].rearrange("p (m t e) -> p t m e", t=PACK, e=2),
            )
        nc.vector.tensor_copy(out=wa_s[:], in_=wa_sraw[:].rearrange("p a (m t) -> p a t m", t=PACK))
        nc.vector.tensor_copy(v_s[:], tab_s[:].indirect(idx1[:]))
        nc.vector.tensor_copy(v_w[0][:], tab_w[0][:].indirect(idx1[:]))
        w1_q = {}
        for a in range(2):
            w1_q[a, 0] = quantised_weight("w1_%d0" % a, w1[a * K_PASS : (a + 1) * K_PASS, 0:K_PASS])
        load_table(1)
        nc.vector.tensor_copy(v_w[1][:], tab_w[1][:].indirect(idx1[:]))
        nc.sync.dma_start(idx2[:], offs2)
        nc.sync.dma_start(out=b1_sb[:], in_=b1.rearrange("(b p t) -> p b t", b=2, t=PACK))

        wb_q = {}
        olds = {}
        for s in range(8):
            b, t = divmod(s, PACK)
            for ahead in {0: (0,), 1: (1, 2), 7: ()}.get(s, (s + 1,)):
                load_page(ahead)
                olds[ahead] = ring.tile([P, S], F32, name="old", tag="picked", bufs=2, align_bytes=64)
                nc.vector.tensor_copy(olds[ahead][:], pages[ahead][:].indirect(idx2[:]))
            old = olds[s]
            ch = ring.tile([P, S], F32, name="ch", tag="ch", bufs=4)
            rows = crowd[b * K_PASS : (b + 1) * K_PASS, :].rearrange("(p t) c -> p t c", t=PACK)
            nc.sync.dma_start(out=ch[:], in_=rows[:, t, :])
            if s > 0:
                h = ring.tile([P, S], F32, name="h", tag="h", bufs=2)
            for j0 in range(0, S, BANK):
                cols = slice(j0, j0 + BANK)
                acc = psum.tile([P, BANK], F32, name="acc", tag="acc")
                for a in range(2):
                    codes, scales = w1_q[a, b]
                    nc.tensor.matmul_mx(
                        out=acc[:],
                        lhsT=codes[:, t * P : (t + 1) * P].bitcast(FP8X4),
                        lhsT_scale=scales[:, t * P : (t + 1) * P],
                        rhs=v_w[a][:, cols].bitcast(FP8X4),
                        rhs_scale=v_s[4 * a :, cols],
                        start=(a == 0),
                        stop=(a == 1),
                    )
                if s == 0:
                    nc.vector.scalar_tensor_tensor(
                        out=ch[:, cols], in0=acc[:], scalar=b1_sb[:, b, t : t + 1], in1=ch[:, cols],
                        op0=ALU.add, op1=ALU.mult,
                    )
                else:
                    nc.scalar.activation(out=h[:, cols], in_=acc[:], func=ACT.Identity, bias=b1_sb[:, b, t : t + 1])
            if s == 0:
                nc.vector.tensor_tensor(pages[s][:].indirect(idx2[:]), old[:], ch[:], ALU.add)
            else:
                nc.gpsimd.tensor_tensor(ch[:], h[:], ch[:], ALU.mult)
                nc.gpsimd.tensor_tensor(ch[:], old[:], ch[:], ALU.add)
                nc.vector.tensor_copy(pages[s][:].indirect(idx2[:]), ch[:])
            if s == 2:
                for a in range(2):
                    w1_q[a, 1] = quantised_weight("w1_%d1" % a, w1[a * K_PASS : (a + 1) * K_PASS, K_PASS:])
            if s == 5:
                nc.sync.dma_start(idx3[:], offs3)
                nc.sync.dma_start(out=ba_sb[:], in_=ba.rearrange("(p t) -> p t", t=PACK))
                nc.sync.dma_start(out=cap_sb[:], in_=cap.rearrange("(p t) -> p t", t=PACK))
                for a in range(2):
                    wb_q[a] = quantised_weight("wb_%d" % a, wb[a * K_PASS : (a + 1) * K_PASS, :])

        out_rows = out_0.rearrange("(p t) m -> p t m", t=PACK)
        out_words = out_1[0].rearrange("p m t -> p (m t)").bitcast(I32)
        out_scales = out_2[0].bitcast(I32)
        m0 = 0
        for w in CHUNKS:
            cols = slice(m0, m0 + w)
            banks = [psum.tile([P, 2, w], F32, name="acc", tag="acc") for t in range(PACK)]
            for b in range(2):
                x = ring.tile([P, PACK, w], BF16, name="x", tag="picked", bufs=2, align_bytes=64)
                for t in range(PACK):
                    nc.vector.tensor_copy(
                        x[:, t, :], pages[PACK * b + t][:].indirect(idx3[:, m0 // PER_COL : (m0 + w) // PER_COL])
                    )
                x_grouped = ring.tile([P, w * PACK], BF16, name="x_grouped", tag="x_grouped", bufs=2, align_bytes=64)
                nc.scalar.copy(
                    out=x_grouped[:].rearrange("p (c i t) -> p c t i", i=4, t=PACK),
                    in_=x[:].rearrange("p t (c i) -> p c t i", i=4),
                )
                x_w = ring.tile([P, w], U32, name="x_w", tag="x_w", bufs=3, align_bytes=64)
                x_s = ring.tile([P, w], U8, name="x_s", tag="x_s", bufs=3, align_bytes=64)
                nc.vector.quantize_mx(out=x_w[:].bitcast(FP8X4), scales=x_s[:], in_=x_grouped[:])
                codes, scales = wb_q[b]
                for t in range(PACK):
                    nc.tensor.matmul_mx(
                        out=banks[t][:, 0, :],
                        lhsT=codes[:, t * P : (t + 1) * P].bitcast(FP8X4),
                        lhsT_scale=scales[:, t * P : (t + 1) * P],
                        rhs=x_w[:].bitcast(FP8X4),
                        rhs_scale=x_s[:],
                        start=(b == 0),
                        stop=False,
                    )
                    nc.tensor.matmul_mx(
                        out=banks[t][:, 1, :],
                        lhsT=wa_w[:, b, t, :].bitcast(FP4X4),
                        lhsT_scale=wa_s[:, b, t, :],
                        rhs=x_w[:].bitcast(FP8X4),
                        rhs_scale=x_s[:],
                        start=False,
                        stop=(b == 1),
                    )
            y = ring.tile([P, PACK, w], F32, name="y", tag="y", bufs=2, align_bytes=64)
            for t in range(PACK):
                yb = ring.tile([P, w], F32, name="yb", tag="yb", bufs=4)
                nc.scalar.activation(out=yb[:], in_=banks[t][:, 0, :], func=ACT.Tanh)
                nc.scalar.activation(out=yb[:], in_=yb[:], func=ACT.Copy, scale=cap_sb[:, t : t + 1])
                nc.vector.scalar_tensor_tensor(
                    out=y[:, t, :], in0=banks[t][:, 1, :], scalar=ba_sb[:, t : t + 1], in1=yb[:],
                    op0=ALU.add, op1=ALU.max,
                )
            nc.sync.dma_start(out=out_rows[:, :, cols], in_=y[:])
            y_grouped = ring.tile([P, w * PACK], BF16, name="y_grouped", tag="y_grouped", bufs=2, align_bytes=64)
            nc.scalar.copy(
                out=y_grouped[:].rearrange("p (c i t) -> p c t i", i=4, t=PACK),
                in_=y[:].rearrange("p t (c i) -> p c t i", i=4),
            )
            nc.vector.quantize_mx(out=y_w[:, cols].bitcast(FP8X4), scales=y_s[:, cols], in_=y_grouped[:])
            nc.sync.dma_start(out=out_words[:, cols], in_=y_w[:, cols].bitcast(I32))
            m0 = m0 + w
        for q in range(4):
            queue = nc.scalar if q % 2 else nc.sync
            queue.dma_start(out=out_scales[4 * q : 4 * q + 4, :], in_=y_s[32 * q : 32 * q + 4, :].bitcast(I32))
